import numpy as np
import ml_dtypes


def mxq(x, axis, fmt="e4m3"):
    dtype, down = {"e4m3": (ml_dtypes.float8_e4m3fn, 7), "e5m2": (ml_dtypes.float8_e5m2, 14)}[fmt]
    v = np.moveaxis(np.asarray(x, np.float32).astype(ml_dtypes.bfloat16).astype(np.float64), axis, -1)
    blocks = v.reshape(v.shape[:-1] + (-1, 32))
    amax = np.abs(blocks).max(-1, keepdims=True)
    byte = np.maximum(np.where(amax > 0, np.frexp(amax)[1] - 1 + 127, 0) - down, 1)
    scale = np.exp2(byte - 127.0)
    codes = (blocks / scale).astype(np.float32).astype(dtype).astype(np.float64)
    return np.moveaxis((codes * scale).reshape(v.shape), -1, axis)


WIDE = False


def mx_kscale(k):
    if not WIDE:
        return np.ones(k)
    levels = np.array([10, -10, 5, -5, 0])
    if k % 512:
        return np.exp2(np.random.permutation(np.resize(levels, k // 32))).repeat(32)
    a = np.empty((k // 512, 16))
    for p in range(k // 512):
        a[p, :8] = np.random.permutation(np.resize(levels, 8))
        for g in range(8):
            far = levels[np.abs(levels - a[p, g]) >= 10]
            a[p, g + 8] = far[np.random.randint(len(far))]
    return np.exp2(a.ravel()).repeat(32)


def f64(x):
    return np.asarray(x).astype(np.float64)


def striped(idx):
    return np.tile(idx.reshape(-1, 16).T, (8, 1)).astype(np.uint16)


def unstriped(offs):
    return offs[:16].T.reshape(-1).astype(np.int64)


E2M1 = np.array([0.0, 0.5, 1.0, 1.5, 2.0, 3.0, 4.0, 6.0, -0.0, -0.5, -1.0, -1.5, -2.0, -3.0, -4.0, -6.0])


def pack_weight(w, fmt):
    k, n = w.shape
    w = f64(np.asarray(w, np.float32).astype(ml_dtypes.bfloat16)).reshape(k // 32, 32, n)
    amax = np.abs(w).max(1)
    if fmt == "e4m3":
        byte = np.frexp(amax)[1] - 1 + 127 - 7
    else:
        mant, ex = np.frexp(amax / 6.0)
        byte = np.where(mant > 0.5, ex, ex - 1) + 127
    byte = np.clip(np.where(amax > 0, byte, 1), 1, 254)
    scaled = (w * np.exp2(127.0 - byte)[:, None, :]).reshape(k, n).astype(np.float32)
    by_word = np.ascontiguousarray(scaled.reshape(k // 512, 128, 4, n).transpose(0, 1, 3, 2))
    if fmt == "e4m3":
        words = by_word.astype(ml_dtypes.float8_e4m3fn).view(np.uint8)
    else:
        c = by_word.astype(ml_dtypes.float4_e2m1fn).view(np.uint8) & 0xF
        words = (c[..., 0::2] | (c[..., 1::2] << 4)).reshape(k // 512, 128, 2 * n)
    return np.ascontiguousarray(words), np.ascontiguousarray(byte.astype(np.uint8).reshape(k // 512, 16, n))


def unpack_weight(words, scales, fmt):
    g, _, n = scales.shape
    words = np.ascontiguousarray(words).reshape(g, 128, n, -1)
    if fmt == "e4m3":
        vals = words.view(ml_dtypes.float8_e4m3fn).astype(np.float64)
    else:
        nib = np.empty((g, 128, n, 4), np.uint8)
        nib[..., 0::2] = words & 0xF
        nib[..., 1::2] = words >> 4
        vals = E2M1[nib]
    vals = vals * np.repeat(np.exp2(scales.astype(np.float64) - 127.0), 8, axis=1)[..., None]
    return vals.transpose(0, 1, 3, 2).reshape(g * 512, n)


def gelu(v):
    return 0.5 * v * (1.0 + np.tanh(np.sqrt(2.0 / np.pi) * (v + 0.044715 * v**3)))


K, H, N, T, S, T2 = 1024, 1024, 384, 4096, 1024, 2048

def setup_inputs():
    n = np.random.standard_normal
    s = mx_kscale(K)[:, None]
    u = mx_kscale(H)[:, None]
    tab_words, tab_scales = pack_weight(n((K, T)) * s, "e4m3")
    wa_words, wa_scales = pack_weight(n((K, H)) * 1.1 / np.sqrt(K) / s, "e2m1")
    return {
        "tab_words": tab_words, "tab_scales": tab_scales,
        "offs": striped(np.random.permutation(T)[:S]),
        "offs2": striped(np.random.permutation(T)[:S]),
        "offs3": striped(np.random.permutation(T2)[:S]),
        "wa_words": wa_words, "wa_scales": wa_scales,
        "wb": (n((K, H)) * 0.52 / np.sqrt(K) / s).astype(np.float32),
        "gain": (np.exp(0.3 * n(H)) * u[:, 0]).astype(np.float32),
        "wc": (n((H, N)) * 2.0 / np.sqrt(H) / u).astype(np.float32),
        "base": (0.5 * n(N)).astype(np.float32),
        "wgo": np.exp(0.3 * n((128, S))).astype(np.float32),
    }

def reference(tab_words, tab_scales, offs, offs2, offs3, wa_words, wa_scales, wb, gain, wc, base, wgo):
    TW = unpack_weight(tab_words, tab_scales, "e4m3")
    v = TW[:, unstriped(offs)]
    v2 = TW[:, unstriped(offs2)]
    wa = unpack_weight(wa_words, wa_scales, "e2m1")
    barge = wa.T @ v
    boat = mxq(f64(wb), 0, "e4m3").T @ v2
    lead = np.tanh(np.maximum(barge, boat))
    z = f64(gain)[:, None] * (lead - np.sin(boat))
    y = mxq(f64(wc), 0, "e4m3").T @ mxq(z, 0, "e4m3")
    y = np.maximum(y, f64(base)[:, None])
    out = np.zeros((N, T2))
    out[:, unstriped(offs3)] = np.tile(f64(wgo), (N // 128, 1)) * y
    return out

@@ -1,0 +1,327 @@
+from contextlib import ExitStack
+
+import concourse.mybir as mybir
+from concourse.masks import make_identity
+
+K, H, N, T, S, T2 = 1024, 1024, 384, 4096, 1024, 2048
+FLOPS = 2 * K * H * S * 2 + 2 * H * N * S
+
+F32 = mybir.dt.float32
+BF16 = mybir.dt.bfloat16
+I32 = mybir.dt.int32
+U32 = mybir.dt.uint32
+U16 = mybir.dt.uint16
+U8 = mybir.dt.uint8
+FP8X4 = mybir.dt.float8_e4m3fn_x4
+FP4X4 = mybir.dt.float4_e2m1fn_x4
+ALU = mybir.AluOpType
+ACT = mybir.ActivationFunctionType
+
+P = 128
+PACK = 4
+PASS = P * PACK
+HALF = 512
+CHUNK = 256
+
+
+def tile_list_tow_plan_features_kernel(
+    tc, tab_words, tab_scales, offs, offs2, offs3, wa_words, wa_scales, wb, gain, wc, base, wgo, out
+):
+    nc = tc.nc
+    with ExitStack() as ctx:
+        held = ctx.enter_context(tc.tile_pool(name="held", bufs=1))
+        ring = ctx.enter_context(tc.tile_pool(name="ring", bufs=3))
+        psum = ctx.enter_context(tc.psum_pool(name="psum", bufs=1))
+
+        def keep(name, shape, dtype):
+            return held.tile(shape, dtype, name=name, align_bytes=64)
+
+        barge_list = held.tile([P, S // 16], U16, name="barge_list")
+        boat_list = held.tile([P, S // 16], U16, name="boat_list")
+        place_list = held.tile([P, S // 16], U16, name="place_list")
+        tab_scale = keep("tab_scale", [P, T], U8)
+        wa_scale = keep("wa_scale", [P, 2, H], U8)
+        barge_scale1 = keep("barge_scale1", [P, S], U8)
+        nc.vector.memset(tab_scale[:].bitcast(I32), 0)
+        nc.sync.dma_start(barge_list[:], offs)
+        nc.sync.dma_start(boat_list[:], offs2)
+        gain_sb = keep("gain_sb", [P, 2, PACK], F32)
+        base_sb = keep("base_sb", [P, 3], F32)
+        nc.vector.memset(wa_scale[:].bitcast(I32), 0)
+        nc.vector.memset(barge_scale1[:].bitcast(I32), 0)
+        pages = [keep("page%d" % i, [P, T2], F32) for i in range(3)]
+        for page in pages:
+            nc.vector.memset(page[:], 0.0)
+        ident = keep("ident", [P, P], F32)
+        make_identity(nc, ident[:])
+
+        tab_word = [keep("tab_word%d" % a, [P, T], I32) for a in range(2)]
+        wb_raw = {(a, g): keep("wb_raw%d%d" % (a, g), [P, PACK, HALF], F32) for a in range(2) for g in range(2)}
+        wc_raw = [keep("wc_raw%d" % g, [P, PACK, N], F32) for g in range(2)]
+        wa_word = keep("wa_word", [P, 2, 2 * H], U8)
+        wgo_sb = keep("wgo_sb", [P, S], F32)
+
+        def load_tab(a):
+            nc.sync.dma_start(out=tab_word[a][:], in_=tab_words[a].rearrange("p t i -> p (t i)").bitcast(I32))
+
+        def load_wb(a, g):
+            rows = wb[a * PASS : (a + 1) * PASS, g * HALF : (g + 1) * HALF]
+            nc.sync.dma_start(out=wb_raw[a, g][:], in_=rows.rearrange("(p j) c -> p j c", j=PACK))
+
+        def load_wc(g):
+            rows = wc[g * PASS : (g + 1) * PASS, :]
+            nc.sync.dma_start(out=wc_raw[g][:], in_=rows.rearrange("(p j) c -> p j c", j=PACK))
+
+        nc.sync.dma_start(out=gain_sb[:], in_=gain.rearrange("(g p t) -> p g t", g=2, t=PACK))
+        for q in range(4):
+            nc.sync.dma_start(
+                out=tab_scale[32 * q : 32 * q + 8, :].bitcast(I32),
+                in_=tab_scales[:, 4 * q : 4 * q + 4, :].bitcast(I32),
+            )
+        load_tab(0)
+        load_wb(0, 0)
+        for q in range(4):
+            nc.sync.dma_start(
+                out=wa_scale[32 * q : 32 * q + 4, :, :].bitcast(I32),
+                in_=wa_scales[:, 4 * q : 4 * q + 4, :].rearrange("a r c -> r a c").bitcast(I32),
+            )
+        load_tab(1)
+        load_wb(1, 0)
+        nc.sync.dma_start(out=wa_word[:].bitcast(I32), in_=wa_words.rearrange("a p c -> p a c").bitcast(I32))
+        load_wb(0, 1)
+        load_wb(1, 1)
+        load_wc(0)
+        load_wc(1)
+        nc.sync.dma_start(place_list[:], offs3)
+        with nc.allow_non_contiguous_dma(reason="one value of base to a partition"):
+            nc.sync.dma_start(out=base_sb[:], in_=base.rearrange("(i p) -> p i", p=P))
+        nc.sync.dma_start(out=wgo_sb[:], in_=wgo)
+
+        barge_scale = keep("barge_scale", [P, S], U8)
+        boat_scale = keep("boat_scale", [P, S], U8)
+        nc.vector.tensor_copy(barge_scale[:], tab_scale[:].indirect(barge_list[:]))
+        nc.vector.tensor_copy(boat_scale[:], tab_scale[:].indirect(boat_list[:]))
+        for q in range(4):
+            nc.scalar.dma_start(
+                out=barge_scale1[32 * q : 32 * q + 4, :].bitcast(I32),
+                in_=barge_scale[32 * q + 4 : 32 * q + 8, :].bitcast(I32),
+            )
+        neg_base = keep("neg_base", [P, 3], F32)
+        nc.scalar.activation(out=neg_base[:], in_=base_sb[:], func=ACT.Copy, scale=-1.0)
+
+        barge_word = {}
+        boat_word = {}
+
+        def gather_words(a, h):
+            cols = slice(h * HALF // 16, (h + 1) * HALF // 16)
+            barge_word[a, h] = keep("barge_word%d%d" % (a, h), [P, HALF], U32)
+            boat_word[a, h] = keep("boat_word%d%d" % (a, h), [P, HALF], U32)
+            window = tab_word[a][:].bitcast(U32)
+            nc.vector.tensor_copy(boat_word[a, h][:], window.indirect(boat_list[:, cols]))
+            nc.vector.tensor_copy(barge_word[a, h][:], window.indirect(barge_list[:, cols]))
+
+        def quantise_weight(name, raw, width, copy):
+            woven = ring.tile([P, HALF, PACK], BF16, name="woven", align_bytes=64)
+            copy(
+                out=woven[:, :width, :].rearrange("p (c i) t -> p c t i", i=4),
+                in_=raw[:].rearrange("p t (c i) -> p c t i", i=4),
+            )
+            codes = keep(name + "_codes", [P, width], U32)
+            scale = keep(name + "_scale", [P, width], U8)
+            nc.vector.quantize_mx(
+                out=codes[:].bitcast(FP8X4),
+                scales=scale[:],
+                in_=woven[:, :width, :].rearrange("p c t -> p (c t)"),
+            )
+            return codes, scale
+
+        boat_banks = [psum.tile([P, HALF], F32, name="boat%d" % b) for b in range(2)]
+        barge_banks = [psum.tile([P, HALF], F32, name="barge%d" % b) for b in range(3)]
+        diff_banks = [psum.tile([P, HALF], F32, name="diff%d" % b) for b in range(3)]
+        y_banks = [psum.tile([P, HALF], F32, name="y%d" % b) for b in range(0)]
+        turn = {"boat": 0, "barge": 0, "diff": 0, "y": 0}
+
+        def take(kind, banks):
+            turn[kind] = turn[kind] + 1
+            return banks[(turn[kind] - 1) % len(banks)]
+
+        held_a = {}
+        held_b = {}
+        wb_q = {}
+        wc_q = {}
+        z_bf = {}
+        z_q = {}
+
+        def products(st, g):
+            h, c0 = divmod(st * P, HALF)
+            tok = slice(c0, c0 + P)
+            tok_all = slice(st * P, (st + 1) * P)
+            boat = take("boat", boat_banks)
+            for a in range(2):
+                codes, scale = wb_q[a, g]
+                nc.tensor.matmul_mx(
+                    out=boat[:],
+                    lhsT=boat_word[a, h][:, tok].bitcast(FP8X4),
+                    lhsT_scale=boat_scale[4 * a : P, tok_all],
+                    rhs=codes[:].bitcast(FP8X4),
+                    rhs_scale=scale[:],
+                    start=(a == 0),
+                    stop=(a == 1),
+                )
+            barge = take("barge", barge_banks)
+            for a in range(2):
+                plane = barge_scale if a == 0 else barge_scale1
+                nc.tensor.matmul_mx(
+                    out=barge[:],
+                    lhsT=barge_word[a, h][:, tok].bitcast(FP8X4),
+                    lhsT_scale=plane[:, tok_all],
+                    rhs=wa_word[:, a, 2 * g * HALF : 2 * (g + 1) * HALF].bitcast(FP4X4),
+                    rhs_scale=wa_scale[:, a, g * HALF : (g + 1) * HALF],
+                    start=(a == 0),
+                    stop=(a == 1),
+                )
+            dealt_boat = boat[:].rearrange("s (m t) -> s t m", t=PACK)
+            dealt_barge = barge[:].rearrange("s (m t) -> s t m", t=PACK)
+            boat_sb = ring.tile([P, PACK, P], F32, name="boat_sb")
+            nc.scalar.copy(out=boat_sb[:], in_=dealt_boat)
+            neg_sine = ring.tile([P, PACK, P], F32, name="neg_sine")
+            nc.scalar.activation(out=neg_sine[:], in_=dealt_boat, func=ACT.Sin, scale=-1.0)
+            held_a[st, g] = (dealt_barge, boat_sb, neg_sine)
+
+        def bend(st, g):
+            dealt_barge, boat_sb, neg_sine = held_a[st, g]
+            larger = ring.tile([P, PACK, P], F32, name="larger")
+            nc.vector.tensor_tensor(out=larger[:], in0=dealt_barge, in1=boat_sb[:], op=ALU.max)
+            lead = ring.tile([P, PACK, P], F32, name="lead")
+            nc.scalar.activation(out=lead[:], in_=larger[:], func=ACT.Tanh)
+            diff = take("diff", diff_banks)[:].rearrange("p (t s) -> p t s", t=PACK)
+            for i, term in enumerate((lead, neg_sine)):
+                for t in range(PACK):
+                    nc.tensor.matmul(
+                        out=diff[:, t, :],
+                        lhsT=term[:, t, :],
+                        rhs=ident[:],
+                        is_transpose=True,
+                        start=(i == 0 and t == 0),
+                        stop=(i == 1 and t == PACK - 1),
+                    )
+            held_b[st, g] = diff
+
+        def scale_z(st, g):
+            diff = held_b[st, g]
+            c, j = divmod(st, CHUNK // P)
+            if j == 0:
+                z_bf[c, g] = ring.tile([P, CHUNK, PACK], BF16, name="z_bf", align_bytes=64, bufs=4)
+            nc.vector.tensor_tensor(
+                out=z_bf[c, g][:, j * P : (j + 1) * P, :],
+                in0=diff.rearrange("p t s -> p s t"),
+                in1=gain_sb[:, g, :].unsqueeze(1).to_broadcast([P, P, PACK]),
+                op=ALU.mult,
+            )
+            if j == CHUNK // P - 1:
+                codes = ring.tile([P, CHUNK], U32, name="z_codes", align_bytes=64, bufs=4)
+                scale = ring.tile([P, CHUNK], U8, name="z_scale", align_bytes=64, bufs=4)
+                nc.vector.quantize_mx(
+                    out=codes[:].bitcast(FP8X4),
+                    scales=scale[:],
+                    in_=z_bf[c, g][:].rearrange("p s t -> p (s t)"),
+                )
+                z_q[c, g] = (codes, scale)
+
+        def finish(c, i):
+            tok = slice(c * CHUNK, (c + 1) * CHUNK)
+            cols = slice(c * CHUNK // 16, (c + 1) * CHUNK // 16)
+            y = take("barge", barge_banks)[:, :CHUNK]
+            for g in range(2):
+                w_codes, w_scale = wc_q[g]
+                codes, scale = z_q[c, g]
+                nc.tensor.matmul_mx(
+                    out=y,
+                    lhsT=w_codes[:, i * P : (i + 1) * P].bitcast(FP8X4),
+                    lhsT_scale=w_scale[:, i * P : (i + 1) * P],
+                    rhs=codes[:].bitcast(FP8X4),
+                    rhs_scale=scale[:],
+                    start=(g == 0),
+                    stop=(g == 1),
+                )
+            feat = ring.tile([P, CHUNK], F32, name="feat", bufs=4)
+            above = ring.tile([P, CHUNK], F32, name="above")
+            nc.scalar.activation(out=above[:], in_=y, func=ACT.Relu, bias=neg_base[:, i : i + 1])
+            nc.scalar.activation(out=feat[:], in_=above[:], func=ACT.Identity, bias=base_sb[:, i : i + 1])
+            nc.vector.tensor_tensor(
+                out=pages[i][:].indirect(place_list[:, cols]), in0=feat[:], in1=wgo_sb[:, tok], op=ALU.mult
+            )
+
+        gather_words(0, 0)
+        wb_q[0, 0] = quantise_weight("wb00", wb_raw[0, 0], HALF, nc.scalar.copy)
+        gather_words(0, 1)
+        gather_words(1, 0)
+        wb_q[1, 0] = quantise_weight("wb10", wb_raw[1, 0], HALF, nc.scalar.copy)
+        gather_words(1, 1)
+        wb_q[0, 1] = quantise_weight("wb01", wb_raw[0, 1], HALF, nc.vector.tensor_copy)
+        wb_q[1, 1] = quantise_weight("wb11", wb_raw[1, 1], HALF, nc.vector.tensor_copy)
+        products(0, 0)
+        products(1, 0)
+        bend(0, 0)
+        wc_q[0] = quantise_weight("wc0", wc_raw[0], N, nc.vector.tensor_copy)
+        products(2, 0)
+        bend(1, 0)
+        scale_z(0, 0)
+        wc_q[1] = quantise_weight("wc1", wc_raw[1], N, nc.vector.tensor_copy)
+        products(0, 1)
+        bend(2, 0)
+        scale_z(1, 0)
+        products(1, 1)
+        bend(0, 1)
+        scale_z(2, 0)
+        products(3, 0)
+        bend(1, 1)
+        scale_z(0, 1)
+        products(2, 1)
+        bend(3, 0)
+        scale_z(1, 1)
+        products(3, 1)
+        bend(2, 1)
+        scale_z(3, 0)
+        finish(0, 0)
+        products(4, 0)
+        bend(3, 1)
+        scale_z(2, 1)
+        finish(0, 1)
+        products(5, 0)
+        bend(4, 0)
+        scale_z(3, 1)
+        finish(0, 2)
+        products(4, 1)
+        bend(5, 0)
+        scale_z(4, 0)
+        finish(1, 0)
+        products(5, 1)
+        bend(4, 1)
+        scale_z(5, 0)
+        finish(1, 1)
+        products(6, 0)
+        bend(5, 1)
+        scale_z(4, 1)
+        finish(1, 2)
+        products(7, 0)
+        bend(6, 0)
+        scale_z(5, 1)
+        products(6, 1)
+        bend(7, 0)
+        scale_z(6, 0)
+        finish(2, 0)
+        products(7, 1)
+        bend(6, 1)
+        scale_z(7, 0)
+        bend(7, 1)
+        scale_z(6, 1)
+        scale_z(7, 1)
+        finish(2, 1)
+        finish(3, 0)
+        finish(3, 1)
+        finish(2, 2)
+        finish(3, 2)
+        nc.sync.dma_start(out=out[0 * P : (0 + 1) * P, :], in_=pages[0][:])
+        nc.sync.dma_start(out=out[1 * P : (1 + 1) * P, :], in_=pages[1][:])
+        nc.sync.dma_start(out=out[2 * P : (2 + 1) * P, :], in_=pages[2][:])

@@ -42,6 +42,10 @@ def tile_list_tow_plan_features_kernel(
         tab_scale = keep("tab_scale", [P, T], U8)
         wa_scale = keep("wa_scale", [P, 2, H], U8)
         barge_scale1 = keep("barge_scale1", [P, S], U8)
+        warm_in = keep("warm_in", [P, 8], F32)
+        warm_out = keep("warm_out", [P, 8], F32)
+        nc.gpsimd.memset(warm_in[:], 0.0)
+        nc.scalar.activation(out=warm_out[:], in_=warm_in[:], func=ACT.Silu)
         nc.vector.memset(tab_scale[:].bitcast(I32), 0)
         nc.sync.dma_start(barge_list[:], offs)
         nc.sync.dma_start(boat_list[:], offs2)
@@ -183,17 +187,18 @@ def tile_list_tow_plan_features_kernel(
             dealt_boat = boat[:].rearrange("s (m t) -> s t m", t=PACK)
             dealt_barge = barge[:].rearrange("s (m t) -> s t m", t=PACK)
             boat_sb = ring.tile([P, PACK, P], F32, name="boat_sb")
-            nc.scalar.copy(out=boat_sb[:], in_=dealt_boat)
+            nc.scalar.activation(out=boat_sb[:], in_=dealt_boat, func=ACT.Tanh)
             neg_sine = ring.tile([P, PACK, P], F32, name="neg_sine")
             nc.scalar.activation(out=neg_sine[:], in_=dealt_boat, func=ACT.Sin, scale=-1.0)
-            held_a[st, g] = (dealt_barge, boat_sb, neg_sine)
+            barge_sb = ring.tile([P, PACK, P], F32, name="barge_sb")
+            nc.scalar.activation(out=barge_sb[:], in_=dealt_barge, func=ACT.Tanh)
+            held_a[st, g] = (barge_sb[:], boat_sb, neg_sine)
 
         def bend(st, g):
             dealt_barge, boat_sb, neg_sine = held_a[st, g]
             larger = ring.tile([P, PACK, P], F32, name="larger")
             nc.vector.tensor_tensor(out=larger[:], in0=dealt_barge, in1=boat_sb[:], op=ALU.max)
-            lead = ring.tile([P, PACK, P], F32, name="lead")
-            nc.scalar.activation(out=lead[:], in_=larger[:], func=ACT.Tanh)
+            lead = larger
             diff = take("diff", diff_banks)[:].rearrange("p (t s) -> p t s", t=PACK)
             for i, term in enumerate((lead, neg_sine)):
                 for t in range(PACK):
@@ -257,26 +262,26 @@ def tile_list_tow_plan_features_kernel(
         gather_words(0, 1)
         gather_words(1, 0)
         wb_q[1, 0] = quantise_weight("wb10", wb_raw[1, 0], HALF, nc.scalar.copy)
-        gather_words(1, 1)
         wb_q[0, 1] = quantise_weight("wb01", wb_raw[0, 1], HALF, nc.vector.tensor_copy)
         wb_q[1, 1] = quantise_weight("wb11", wb_raw[1, 1], HALF, nc.vector.tensor_copy)
         products(0, 0)
+        gather_words(1, 1)
         products(1, 0)
         bend(0, 0)
-        wc_q[0] = quantise_weight("wc0", wc_raw[0], N, nc.vector.tensor_copy)
         products(2, 0)
         bend(1, 0)
         scale_z(0, 0)
-        wc_q[1] = quantise_weight("wc1", wc_raw[1], N, nc.vector.tensor_copy)
         products(0, 1)
         bend(2, 0)
         scale_z(1, 0)
         products(1, 1)
         bend(0, 1)
         scale_z(2, 0)
+        wc_q[0] = quantise_weight("wc0", wc_raw[0], N, nc.vector.tensor_copy)
         products(3, 0)
         bend(1, 1)
         scale_z(0, 1)
+        wc_q[1] = quantise_weight("wc1", wc_raw[1], N, nc.vector.tensor_copy)
         products(2, 1)
         bend(3, 0)
         scale_z(1, 1)

@@ -49,6 +49,7 @@ def tile_list_tow_plan_features_kernel(
         nc.vector.memset(tab_scale[:].bitcast(I32), 0)
         nc.sync.dma_start(barge_list[:], offs)
         nc.sync.dma_start(boat_list[:], offs2)
+        nc.sync.dma_start(place_list[:], offs3)
         gain_sb = keep("gain_sb", [P, 2, PACK], F32)
         base_sb = keep("base_sb", [P, 3], F32)
         nc.vector.memset(wa_scale[:].bitcast(I32), 0)
@@ -60,7 +61,8 @@ def tile_list_tow_plan_features_kernel(
         make_identity(nc, ident[:])
 
         tab_word = [keep("tab_word%d" % a, [P, T], I32) for a in range(2)]
-        wb_raw = {(a, g): keep("wb_raw%d%d" % (a, g), [P, PACK, HALF], F32) for a in range(2) for g in range(2)}
+        wb_raw = {(a, g): keep("wb_raw%d%d" % (a, g), [P, PACK, HALF], F32) for a in range(2) for g in range(2) if (a, g) != (1, 0)}
+        wb_raw[1, 0] = held.tile([P, PACK, HALF], F32, name="wb_raw10b", tag="late", align_bytes=64)
         wc_raw = [keep("wc_raw%d" % g, [P, PACK, N], F32) for g in range(2)]
         wa_word = keep("wa_word", [P, 2, 2 * H], U8)
         wgo_sb = keep("wgo_sb", [P, S], F32)
@@ -76,27 +78,32 @@ def tile_list_tow_plan_features_kernel(
             rows = wc[g * PASS : (g + 1) * PASS, :]
             nc.sync.dma_start(out=wc_raw[g][:], in_=rows.rearrange("(p j) c -> p j c", j=PACK))
 
-        nc.sync.dma_start(out=gain_sb[:], in_=gain.rearrange("(g p t) -> p g t", g=2, t=PACK))
-        for q in range(4):
-            nc.sync.dma_start(
-                out=tab_scale[32 * q : 32 * q + 8, :].bitcast(I32),
-                in_=tab_scales[:, 4 * q : 4 * q + 4, :].bitcast(I32),
-            )
+        for a in range(2):
+            for q in range(4):
+                nc.sync.dma_start(
+                    out=tab_scale[32 * q + 4 * a : 32 * q + 4 * a + 4, :].bitcast(I32),
+                    in_=tab_scales[a, 4 * q : 4 * q + 4, :].bitcast(I32),
+                )
         load_tab(0)
         load_wb(0, 0)
-        for q in range(4):
+        load_tab(1)
+        load_wb(1, 0)
+        for q in range(2):
             nc.sync.dma_start(
                 out=wa_scale[32 * q : 32 * q + 4, :, :].bitcast(I32),
                 in_=wa_scales[:, 4 * q : 4 * q + 4, :].rearrange("a r c -> r a c").bitcast(I32),
             )
-        load_tab(1)
-        load_wb(1, 0)
         nc.sync.dma_start(out=wa_word[:].bitcast(I32), in_=wa_words.rearrange("a p c -> p a c").bitcast(I32))
+        for q in range(2, 4):
+            nc.sync.dma_start(
+                out=wa_scale[32 * q : 32 * q + 4, :, :].bitcast(I32),
+                in_=wa_scales[:, 4 * q : 4 * q + 4, :].rearrange("a r c -> r a c").bitcast(I32),
+            )
         load_wb(0, 1)
+        nc.sync.dma_start(out=gain_sb[:], in_=gain.rearrange("(g p t) -> p g t", g=2, t=PACK))
         load_wb(1, 1)
         load_wc(0)
         load_wc(1)
-        nc.sync.dma_start(place_list[:], offs3)
         with nc.allow_non_contiguous_dma(reason="one value of base to a partition"):
             nc.sync.dma_start(out=base_sb[:], in_=base.rearrange("(i p) -> p i", p=P))
         nc.sync.dma_start(out=wgo_sb[:], in_=wgo)
@@ -117,9 +124,21 @@ def tile_list_tow_plan_features_kernel(
         boat_word = {}
 
         def gather_words(a, h):
+            if a == 0:
+                if h == 0:
+                    for words, name, picks in ((boat_word, "boat", boat_list), (barge_word, "barge", barge_list)):
+                        whole = keep(name + "_word0", [P, S], U32)
+                        nc.vector.tensor_copy(whole[:], tab_word[0][:].bitcast(U32).indirect(picks[:]))
+                        words[0, 0] = whole[:, :HALF]
+                        words[0, 1] = whole[:, HALF:]
+                return
             cols = slice(h * HALF // 16, (h + 1) * HALF // 16)
             barge_word[a, h] = keep("barge_word%d%d" % (a, h), [P, HALF], U32)
             boat_word[a, h] = keep("boat_word%d%d" % (a, h), [P, HALF], U32)
+            if (a, h) == (1, 1):
+                both = held.tile([P, 2 * HALF], U32, name="late_words", tag="late", align_bytes=64)
+                boat_word[a, h] = both[:, :HALF]
+                barge_word[a, h] = both[:, HALF:]
             window = tab_word[a][:].bitcast(U32)
             nc.vector.tensor_copy(boat_word[a, h][:], window.indirect(boat_list[:, cols]))
             nc.vector.tensor_copy(barge_word[a, h][:], window.indirect(barge_list[:, cols]))
@@ -215,7 +234,9 @@ def tile_list_tow_plan_features_kernel(
         def scale_z(st, g):
             diff = held_b[st, g]
             c, j = divmod(st, CHUNK // P)
-            if j == 0:
+            if (c, g, j) == (3, 1, 0):
+                z_bf[c, g] = held.tile([P, CHUNK, PACK], BF16, name="tail_z", tag="tail", align_bytes=64)
+            elif j == 0:
                 z_bf[c, g] = ring.tile([P, CHUNK, PACK], BF16, name="z_bf", align_bytes=64, bufs=4)
             nc.vector.tensor_tensor(
                 out=z_bf[c, g][:, j * P : (j + 1) * P, :],
@@ -249,7 +270,16 @@ def tile_list_tow_plan_features_kernel(
                     start=(g == 0),
                     stop=(g == 1),
                 )
-            feat = ring.tile([P, CHUNK], F32, name="feat", bufs=4)
+            if (c, i) == (2, 1):
+                feat = held.tile([P, CHUNK], F32, name="tail_feat", tag="tail", align_bytes=64)
+            else:
+                feat = ring.tile([P, CHUNK], F32, name="feat", bufs=4)
+            if (c, i) == (2, 1):
+                nc.vector.scalar_tensor_tensor(
+                    out=feat[:], in0=y, scalar=base_sb[:, i : i + 1], in1=wgo_sb[:, tok], op0=ALU.max, op1=ALU.mult
+                )
+                nc.vector.tensor_copy(pages[i][:].indirect(place_list[:, cols]), feat[:])
+                return
             above = ring.tile([P, CHUNK], F32, name="above")
             nc.scalar.activation(out=above[:], in_=y, func=ACT.Relu, bias=neg_base[:, i : i + 1])
             nc.scalar.activation(out=feat[:], in_=above[:], func=ACT.Identity, bias=base_sb[:, i : i + 1])
@@ -315,10 +345,10 @@ def tile_list_tow_plan_features_kernel(
         products(6, 1)
         bend(7, 0)
         scale_z(6, 0)
-        finish(2, 0)
         products(7, 1)
         bend(6, 1)
         scale_z(7, 0)
+        finish(2, 0)
         bend(7, 1)
         scale_z(6, 1)
         scale_z(7, 1)

@@ -20,8 +20,14 @@ ACT = mybir.ActivationFunctionType
 P = 128
 PACK = 4
 PASS = P * PACK
-HALF = 512
+PASSES = 2
+HALF = S // 2
 CHUNK = 256
+CHUNKS = S // CHUNK
+PAGES = N // P
+PER_COLUMN = 16
+STREAM_BUFS = 3
+CHUNK_BUFS = 4
 
 
 def tile_list_tow_plan_features_kernel(
@@ -30,81 +36,81 @@ def tile_list_tow_plan_features_kernel(
     nc = tc.nc
     with ExitStack() as ctx:
         held = ctx.enter_context(tc.tile_pool(name="held", bufs=1))
-        ring = ctx.enter_context(tc.tile_pool(name="ring", bufs=3))
+        ring = ctx.enter_context(tc.tile_pool(name="ring", bufs=STREAM_BUFS))
         psum = ctx.enter_context(tc.psum_pool(name="psum", bufs=1))
 
-        def keep(name, shape, dtype):
-            return held.tile(shape, dtype, name=name, align_bytes=64)
+        def keep(name, shape, dtype, tag=""):
+            return held.tile(shape, dtype, name=name, tag=tag or name, align_bytes=64)
 
-        barge_list = held.tile([P, S // 16], U16, name="barge_list")
-        boat_list = held.tile([P, S // 16], U16, name="boat_list")
-        place_list = held.tile([P, S // 16], U16, name="place_list")
+        def list_columns(first, count):
+            return slice(first // PER_COLUMN, (first + count) // PER_COLUMN)
+
+        barge_list = held.tile([P, S // PER_COLUMN], U16, name="barge_list")
+        boat_list = held.tile([P, S // PER_COLUMN], U16, name="boat_list")
+        place_list = held.tile([P, S // PER_COLUMN], U16, name="place_list")
         tab_scale = keep("tab_scale", [P, T], U8)
-        wa_scale = keep("wa_scale", [P, 2, H], U8)
-        barge_scale1 = keep("barge_scale1", [P, S], U8)
+        wa_scale = keep("wa_scale", [P, PASSES, H], U8)
+        barge_scale_pass1 = keep("barge_scale_pass1", [P, S], U8)
+
         warm_in = keep("warm_in", [P, 8], F32)
         warm_out = keep("warm_out", [P, 8], F32)
         nc.gpsimd.memset(warm_in[:], 0.0)
         nc.scalar.activation(out=warm_out[:], in_=warm_in[:], func=ACT.Silu)
+
         nc.vector.memset(tab_scale[:].bitcast(I32), 0)
         nc.sync.dma_start(barge_list[:], offs)
         nc.sync.dma_start(boat_list[:], offs2)
         nc.sync.dma_start(place_list[:], offs3)
-        gain_sb = keep("gain_sb", [P, 2, PACK], F32)
-        base_sb = keep("base_sb", [P, 3], F32)
+        gain_sb = keep("gain_sb", [P, PASSES, PACK], F32)
+        base_sb = keep("base_sb", [P, PAGES], F32)
         nc.vector.memset(wa_scale[:].bitcast(I32), 0)
-        nc.vector.memset(barge_scale1[:].bitcast(I32), 0)
-        pages = [keep("page%d" % i, [P, T2], F32) for i in range(3)]
+        nc.vector.memset(barge_scale_pass1[:].bitcast(I32), 0)
+        pages = [keep("page%d" % i, [P, T2], F32) for i in range(PAGES)]
         for page in pages:
             nc.vector.memset(page[:], 0.0)
         ident = keep("ident", [P, P], F32)
         make_identity(nc, ident[:])
 
-        tab_word = [keep("tab_word%d" % a, [P, T], I32) for a in range(2)]
-        wb_raw = {(a, g): keep("wb_raw%d%d" % (a, g), [P, PACK, HALF], F32) for a in range(2) for g in range(2) if (a, g) != (1, 0)}
-        wb_raw[1, 0] = held.tile([P, PACK, HALF], F32, name="wb_raw10b", tag="late", align_bytes=64)
-        wc_raw = [keep("wc_raw%d" % g, [P, PACK, N], F32) for g in range(2)]
-        wa_word = keep("wa_word", [P, 2, 2 * H], U8)
+        tab_word = [keep("tab_word%d" % a, [P, T], I32) for a in range(PASSES)]
+        wb_raw = {(a, g): keep("wb_raw%d%d" % (a, g), [P, PACK, PASS], F32) for a, g in ((0, 0), (0, 1), (1, 1))}
+        wb_raw[1, 0] = keep("wb_raw10", [P, PACK, PASS], F32, tag="late")
+        wc_raw = [keep("wc_raw%d" % g, [P, PACK, N], F32) for g in range(PASSES)]
+        wa_word = keep("wa_word", [P, PASSES, 2 * H], U8)
         wgo_sb = keep("wgo_sb", [P, S], F32)
 
-        def load_tab(a):
+        def load_tab_words(a):
             nc.sync.dma_start(out=tab_word[a][:], in_=tab_words[a].rearrange("p t i -> p (t i)").bitcast(I32))
 
         def load_wb(a, g):
-            rows = wb[a * PASS : (a + 1) * PASS, g * HALF : (g + 1) * HALF]
-            nc.sync.dma_start(out=wb_raw[a, g][:], in_=rows.rearrange("(p j) c -> p j c", j=PACK))
+            rows = wb[a * PASS : (a + 1) * PASS, g * PASS : (g + 1) * PASS]
+            nc.sync.dma_start(out=wb_raw[a, g][:], in_=rows.rearrange("(p t) c -> p t c", t=PACK))
 
-        def load_wc(g):
-            rows = wc[g * PASS : (g + 1) * PASS, :]
-            nc.sync.dma_start(out=wc_raw[g][:], in_=rows.rearrange("(p j) c -> p j c", j=PACK))
+        def load_wa_scales(quadrants):
+            for q in quadrants:
+                nc.sync.dma_start(
+                    out=wa_scale[32 * q : 32 * q + 4, :, :].bitcast(I32),
+                    in_=wa_scales[:, 4 * q : 4 * q + 4, :].rearrange("a r c -> r a c").bitcast(I32),
+                )
 
-        for a in range(2):
+        for a in range(PASSES):
             for q in range(4):
                 nc.sync.dma_start(
                     out=tab_scale[32 * q + 4 * a : 32 * q + 4 * a + 4, :].bitcast(I32),
                     in_=tab_scales[a, 4 * q : 4 * q + 4, :].bitcast(I32),
                 )
-        load_tab(0)
-        load_wb(0, 0)
-        load_tab(1)
-        load_wb(1, 0)
-        for q in range(2):
-            nc.sync.dma_start(
-                out=wa_scale[32 * q : 32 * q + 4, :, :].bitcast(I32),
-                in_=wa_scales[:, 4 * q : 4 * q + 4, :].rearrange("a r c -> r a c").bitcast(I32),
-            )
+        for a in range(PASSES):
+            load_tab_words(a)
+            load_wb(a, 0)
+        load_wa_scales((0, 1))
         nc.sync.dma_start(out=wa_word[:].bitcast(I32), in_=wa_words.rearrange("a p c -> p a c").bitcast(I32))
-        for q in range(2, 4):
-            nc.sync.dma_start(
-                out=wa_scale[32 * q : 32 * q + 4, :, :].bitcast(I32),
-                in_=wa_scales[:, 4 * q : 4 * q + 4, :].rearrange("a r c -> r a c").bitcast(I32),
-            )
+        load_wa_scales((2, 3))
         load_wb(0, 1)
-        nc.sync.dma_start(out=gain_sb[:], in_=gain.rearrange("(g p t) -> p g t", g=2, t=PACK))
+        nc.sync.dma_start(out=gain_sb[:], in_=gain.rearrange("(g p t) -> p g t", g=PASSES, t=PACK))
         load_wb(1, 1)
-        load_wc(0)
-        load_wc(1)
-        with nc.allow_non_contiguous_dma(reason="one value of base to a partition"):
+        for g in range(PASSES):
+            rows = wc[g * PASS : (g + 1) * PASS, :]
+            nc.sync.dma_start(out=wc_raw[g][:], in_=rows.rearrange("(p t) c -> p t c", t=PACK))
+        with nc.allow_non_contiguous_dma(reason="one value of base to a partition and page"):
             nc.sync.dma_start(out=base_sb[:], in_=base.rearrange("(i p) -> p i", p=P))
         nc.sync.dma_start(out=wgo_sb[:], in_=wgo)
 
@@ -114,37 +120,32 @@ def tile_list_tow_plan_features_kernel(
         nc.vector.tensor_copy(boat_scale[:], tab_scale[:].indirect(boat_list[:]))
         for q in range(4):
             nc.scalar.dma_start(
-                out=barge_scale1[32 * q : 32 * q + 4, :].bitcast(I32),
+                out=barge_scale_pass1[32 * q : 32 * q + 4, :].bitcast(I32),
                 in_=barge_scale[32 * q + 4 : 32 * q + 8, :].bitcast(I32),
             )
-        neg_base = keep("neg_base", [P, 3], F32)
+        neg_base = keep("neg_base", [P, PAGES], F32)
         nc.scalar.activation(out=neg_base[:], in_=base_sb[:], func=ACT.Copy, scale=-1.0)
 
         barge_word = {}
         boat_word = {}
 
-        def gather_words(a, h):
-            if a == 0:
-                if h == 0:
-                    for words, name, picks in ((boat_word, "boat", boat_list), (barge_word, "barge", barge_list)):
-                        whole = keep(name + "_word0", [P, S], U32)
-                        nc.vector.tensor_copy(whole[:], tab_word[0][:].bitcast(U32).indirect(picks[:]))
-                        words[0, 0] = whole[:, :HALF]
-                        words[0, 1] = whole[:, HALF:]
-                return
-            cols = slice(h * HALF // 16, (h + 1) * HALF // 16)
-            barge_word[a, h] = keep("barge_word%d%d" % (a, h), [P, HALF], U32)
-            boat_word[a, h] = keep("boat_word%d%d" % (a, h), [P, HALF], U32)
-            if (a, h) == (1, 1):
-                both = held.tile([P, 2 * HALF], U32, name="late_words", tag="late", align_bytes=64)
-                boat_word[a, h] = both[:, :HALF]
-                barge_word[a, h] = both[:, HALF:]
-            window = tab_word[a][:].bitcast(U32)
-            nc.vector.tensor_copy(boat_word[a, h][:], window.indirect(boat_list[:, cols]))
-            nc.vector.tensor_copy(barge_word[a, h][:], window.indirect(barge_list[:, cols]))
+        def gather_pass0():
+            for words, name, picks in ((boat_word, "boat", boat_list), (barge_word, "barge", barge_list)):
+                whole = keep(name + "_word0", [P, S], U32)
+                nc.vector.tensor_copy(whole[:], tab_word[0][:].bitcast(U32).indirect(picks[:]))
+                words[0, 0] = whole[:, :HALF]
+                words[0, 1] = whole[:, HALF:]
+
+        def gather_pass1(h, boat_into, barge_into):
+            window = tab_word[1][:].bitcast(U32)
+            cols = list_columns(h * HALF, HALF)
+            nc.vector.tensor_copy(boat_into, window.indirect(boat_list[:, cols]))
+            nc.vector.tensor_copy(barge_into, window.indirect(barge_list[:, cols]))
+            boat_word[1, h] = boat_into
+            barge_word[1, h] = barge_into
 
         def quantise_weight(name, raw, width, copy):
-            woven = ring.tile([P, HALF, PACK], BF16, name="woven", align_bytes=64)
+            woven = ring.tile([P, PASS, PACK], BF16, name="woven", align_bytes=64)
             copy(
                 out=woven[:, :width, :].rearrange("p (c i) t -> p c t i", i=4),
                 in_=raw[:].rearrange("p t (c i) -> p c t i", i=4),
@@ -158,67 +159,65 @@ def tile_list_tow_plan_features_kernel(
             )
             return codes, scale
 
-        boat_banks = [psum.tile([P, HALF], F32, name="boat%d" % b) for b in range(2)]
-        barge_banks = [psum.tile([P, HALF], F32, name="barge%d" % b) for b in range(3)]
-        diff_banks = [psum.tile([P, HALF], F32, name="diff%d" % b) for b in range(3)]
-        y_banks = [psum.tile([P, HALF], F32, name="y%d" % b) for b in range(0)]
-        turn = {"boat": 0, "barge": 0, "diff": 0, "y": 0}
+        banks = {
+            kind: [psum.tile([P, PASS], F32, name="%s%d" % (kind, b)) for b in range(count)]
+            for kind, count in (("boat", 2), ("barge", 3), ("diff", 3))
+        }
+        taken = {kind: 0 for kind in banks}
 
-        def take(kind, banks):
-            turn[kind] = turn[kind] + 1
-            return banks[(turn[kind] - 1) % len(banks)]
+        def next_bank(kind):
+            taken[kind] = taken[kind] + 1
+            return banks[kind][(taken[kind] - 1) % len(banks[kind])]
 
-        held_a = {}
-        held_b = {}
         wb_q = {}
         wc_q = {}
+        bent = {}
+        diffs = {}
         z_bf = {}
         z_q = {}
 
         def products(st, g):
-            h, c0 = divmod(st * P, HALF)
-            tok = slice(c0, c0 + P)
-            tok_all = slice(st * P, (st + 1) * P)
-            boat = take("boat", boat_banks)
-            for a in range(2):
+            h, first = divmod(st * P, HALF)
+            in_half = slice(first, first + P)
+            entries = slice(st * P, (st + 1) * P)
+            boat = next_bank("boat")
+            for a in range(PASSES):
                 codes, scale = wb_q[a, g]
                 nc.tensor.matmul_mx(
                     out=boat[:],
-                    lhsT=boat_word[a, h][:, tok].bitcast(FP8X4),
-                    lhsT_scale=boat_scale[4 * a : P, tok_all],
+                    lhsT=boat_word[a, h][:, in_half].bitcast(FP8X4),
+                    lhsT_scale=boat_scale[4 * a : P, entries],
                     rhs=codes[:].bitcast(FP8X4),
                     rhs_scale=scale[:],
                     start=(a == 0),
-                    stop=(a == 1),
+                    stop=(a == PASSES - 1),
                 )
-            barge = take("barge", barge_banks)
-            for a in range(2):
-                plane = barge_scale if a == 0 else barge_scale1
+            barge = next_bank("barge")
+            for a, rows in enumerate((barge_scale, barge_scale_pass1)):
                 nc.tensor.matmul_mx(
                     out=barge[:],
-                    lhsT=barge_word[a, h][:, tok].bitcast(FP8X4),
-                    lhsT_scale=plane[:, tok_all],
-                    rhs=wa_word[:, a, 2 * g * HALF : 2 * (g + 1) * HALF].bitcast(FP4X4),
-                    rhs_scale=wa_scale[:, a, g * HALF : (g + 1) * HALF],
+                    lhsT=barge_word[a, h][:, in_half].bitcast(FP8X4),
+                    lhsT_scale=rows[:, entries],
+                    rhs=wa_word[:, a, 2 * g * PASS : 2 * (g + 1) * PASS].bitcast(FP4X4),
+                    rhs_scale=wa_scale[:, a, g * PASS : (g + 1) * PASS],
                     start=(a == 0),
-                    stop=(a == 1),
+                    stop=(a == PASSES - 1),
                 )
-            dealt_boat = boat[:].rearrange("s (m t) -> s t m", t=PACK)
-            dealt_barge = barge[:].rearrange("s (m t) -> s t m", t=PACK)
-            boat_sb = ring.tile([P, PACK, P], F32, name="boat_sb")
-            nc.scalar.activation(out=boat_sb[:], in_=dealt_boat, func=ACT.Tanh)
+            boat_by_slot = boat[:].rearrange("s (m t) -> s t m", t=PACK)
+            barge_by_slot = barge[:].rearrange("s (m t) -> s t m", t=PACK)
+            tanh_boat = ring.tile([P, PACK, P], F32, name="tanh_boat")
+            nc.scalar.activation(out=tanh_boat[:], in_=boat_by_slot, func=ACT.Tanh)
             neg_sine = ring.tile([P, PACK, P], F32, name="neg_sine")
-            nc.scalar.activation(out=neg_sine[:], in_=dealt_boat, func=ACT.Sin, scale=-1.0)
-            barge_sb = ring.tile([P, PACK, P], F32, name="barge_sb")
-            nc.scalar.activation(out=barge_sb[:], in_=dealt_barge, func=ACT.Tanh)
-            held_a[st, g] = (barge_sb[:], boat_sb, neg_sine)
+            nc.scalar.activation(out=neg_sine[:], in_=boat_by_slot, func=ACT.Sin, scale=-1.0)
+            tanh_barge = ring.tile([P, PACK, P], F32, name="tanh_barge")
+            nc.scalar.activation(out=tanh_barge[:], in_=barge_by_slot, func=ACT.Tanh)
+            bent[st, g] = (tanh_barge, tanh_boat, neg_sine)
 
-        def bend(st, g):
-            dealt_barge, boat_sb, neg_sine = held_a[st, g]
-            larger = ring.tile([P, PACK, P], F32, name="larger")
-            nc.vector.tensor_tensor(out=larger[:], in0=dealt_barge, in1=boat_sb[:], op=ALU.max)
-            lead = larger
-            diff = take("diff", diff_banks)[:].rearrange("p (t s) -> p t s", t=PACK)
+        def difference(st, g):
+            tanh_barge, tanh_boat, neg_sine = bent[st, g]
+            lead = ring.tile([P, PACK, P], F32, name="lead")
+            nc.vector.tensor_tensor(out=lead[:], in0=tanh_barge[:], in1=tanh_boat[:], op=ALU.max)
+            diff = next_bank("diff")[:].rearrange("p (t s) -> p t s", t=PACK)
             for i, term in enumerate((lead, neg_sine)):
                 for t in range(PACK):
                     nc.tensor.matmul(
@@ -229,24 +228,23 @@ def tile_list_tow_plan_features_kernel(
                         start=(i == 0 and t == 0),
                         stop=(i == 1 and t == PACK - 1),
                     )
-            held_b[st, g] = diff
+            diffs[st, g] = diff
 
-        def scale_z(st, g):
-            diff = held_b[st, g]
+        def make_z(st, g):
             c, j = divmod(st, CHUNK // P)
-            if (c, g, j) == (3, 1, 0):
-                z_bf[c, g] = held.tile([P, CHUNK, PACK], BF16, name="tail_z", tag="tail", align_bytes=64)
+            if (c, g, j) == (CHUNKS - 1, PASSES - 1, 0):
+                z_bf[c, g] = keep("last_z_bf", [P, CHUNK, PACK], BF16, tag="tail")
             elif j == 0:
-                z_bf[c, g] = ring.tile([P, CHUNK, PACK], BF16, name="z_bf", align_bytes=64, bufs=4)
+                z_bf[c, g] = ring.tile([P, CHUNK, PACK], BF16, name="z_bf", align_bytes=64, bufs=CHUNK_BUFS)
             nc.vector.tensor_tensor(
                 out=z_bf[c, g][:, j * P : (j + 1) * P, :],
-                in0=diff.rearrange("p t s -> p s t"),
+                in0=diffs[st, g].rearrange("p t s -> p s t"),
                 in1=gain_sb[:, g, :].unsqueeze(1).to_broadcast([P, P, PACK]),
                 op=ALU.mult,
             )
             if j == CHUNK // P - 1:
-                codes = ring.tile([P, CHUNK], U32, name="z_codes", align_bytes=64, bufs=4)
-                scale = ring.tile([P, CHUNK], U8, name="z_scale", align_bytes=64, bufs=4)
+                codes = ring.tile([P, CHUNK], U32, name="z_codes", align_bytes=64, bufs=CHUNK_BUFS)
+                scale = ring.tile([P, CHUNK], U8, name="z_scale", align_bytes=64, bufs=CHUNK_BUFS)
                 nc.vector.quantize_mx(
                     out=codes[:].bitcast(FP8X4),
                     scales=scale[:],
@@ -254,11 +252,9 @@ def tile_list_tow_plan_features_kernel(
                 )
                 z_q[c, g] = (codes, scale)
 
-        def finish(c, i):
-            tok = slice(c * CHUNK, (c + 1) * CHUNK)
-            cols = slice(c * CHUNK // 16, (c + 1) * CHUNK // 16)
-            y = take("barge", barge_banks)[:, :CHUNK]
-            for g in range(2):
+        def last_product(c, i):
+            y = next_bank("barge")[:, :CHUNK]
+            for g in range(PASSES):
                 w_codes, w_scale = wc_q[g]
                 codes, scale = z_q[c, g]
                 nc.tensor.matmul_mx(
@@ -268,95 +264,79 @@ def tile_list_tow_plan_features_kernel(
                     rhs=codes[:].bitcast(FP8X4),
                     rhs_scale=scale[:],
                     start=(g == 0),
-                    stop=(g == 1),
+                    stop=(g == PASSES - 1),
                 )
-            if (c, i) == (2, 1):
-                feat = held.tile([P, CHUNK], F32, name="tail_feat", tag="tail", align_bytes=64)
-            else:
-                feat = ring.tile([P, CHUNK], F32, name="feat", bufs=4)
-            if (c, i) == (2, 1):
-                nc.vector.scalar_tensor_tensor(
-                    out=feat[:], in0=y, scalar=base_sb[:, i : i + 1], in1=wgo_sb[:, tok], op0=ALU.max, op1=ALU.mult
-                )
-                nc.vector.tensor_copy(pages[i][:].indirect(place_list[:, cols]), feat[:])
-                return
+            return y
+
+        def floor_at_base(c, i, into):
+            y = last_product(c, i)
             above = ring.tile([P, CHUNK], F32, name="above")
             nc.scalar.activation(out=above[:], in_=y, func=ACT.Relu, bias=neg_base[:, i : i + 1])
-            nc.scalar.activation(out=feat[:], in_=above[:], func=ACT.Identity, bias=base_sb[:, i : i + 1])
+            nc.scalar.activation(out=into, in_=above[:], func=ACT.Identity, bias=base_sb[:, i : i + 1])
+
+        def scatter(i, first, count, values):
             nc.vector.tensor_tensor(
-                out=pages[i][:].indirect(place_list[:, cols]), in0=feat[:], in1=wgo_sb[:, tok], op=ALU.mult
+                out=pages[i][:].indirect(place_list[:, list_columns(first, count)]),
+                in0=values,
+                in1=wgo_sb[:, first : first + count],
+                op=ALU.mult,
             )
 
-        gather_words(0, 0)
-        wb_q[0, 0] = quantise_weight("wb00", wb_raw[0, 0], HALF, nc.scalar.copy)
-        gather_words(0, 1)
-        gather_words(1, 0)
-        wb_q[1, 0] = quantise_weight("wb10", wb_raw[1, 0], HALF, nc.scalar.copy)
-        wb_q[0, 1] = quantise_weight("wb01", wb_raw[0, 1], HALF, nc.vector.tensor_copy)
-        wb_q[1, 1] = quantise_weight("wb11", wb_raw[1, 1], HALF, nc.vector.tensor_copy)
-        products(0, 0)
-        gather_words(1, 1)
-        products(1, 0)
-        bend(0, 0)
-        products(2, 0)
-        bend(1, 0)
-        scale_z(0, 0)
-        products(0, 1)
-        bend(2, 0)
-        scale_z(1, 0)
-        products(1, 1)
-        bend(0, 1)
-        scale_z(2, 0)
-        wc_q[0] = quantise_weight("wc0", wc_raw[0], N, nc.vector.tensor_copy)
-        products(3, 0)
-        bend(1, 1)
-        scale_z(0, 1)
-        wc_q[1] = quantise_weight("wc1", wc_raw[1], N, nc.vector.tensor_copy)
-        products(2, 1)
-        bend(3, 0)
-        scale_z(1, 1)
-        products(3, 1)
-        bend(2, 1)
-        scale_z(3, 0)
-        finish(0, 0)
-        products(4, 0)
-        bend(3, 1)
-        scale_z(2, 1)
-        finish(0, 1)
-        products(5, 0)
-        bend(4, 0)
-        scale_z(3, 1)
-        finish(0, 2)
-        products(4, 1)
-        bend(5, 0)
-        scale_z(4, 0)
-        finish(1, 0)
-        products(5, 1)
-        bend(4, 1)
-        scale_z(5, 0)
-        finish(1, 1)
-        products(6, 0)
-        bend(5, 1)
-        scale_z(4, 1)
-        finish(1, 2)
-        products(7, 0)
-        bend(6, 0)
-        scale_z(5, 1)
-        products(6, 1)
-        bend(7, 0)
-        scale_z(6, 0)
-        products(7, 1)
-        bend(6, 1)
-        scale_z(7, 0)
-        finish(2, 0)
-        bend(7, 1)
-        scale_z(6, 1)
-        scale_z(7, 1)
-        finish(2, 1)
-        finish(3, 0)
-        finish(3, 1)
-        finish(2, 2)
-        finish(3, 2)
-        nc.sync.dma_start(out=out[0 * P : (0 + 1) * P, :], in_=pages[0][:])
-        nc.sync.dma_start(out=out[1 * P : (1 + 1) * P, :], in_=pages[1][:])
-        nc.sync.dma_start(out=out[2 * P : (2 + 1) * P, :], in_=pages[2][:])
+        def place(c, i):
+            floored = ring.tile([P, CHUNK], F32, name="floored", bufs=CHUNK_BUFS)
+            floor_at_base(c, i, floored[:])
+            scatter(i, c * CHUNK, CHUNK, floored[:])
+
+        def place_from_psum(c, i):
+            y = last_product(c, i)
+            weighted = keep("weighted", [P, CHUNK], F32, tag="tail")
+            nc.vector.scalar_tensor_tensor(
+                out=weighted[:],
+                in0=y,
+                scalar=base_sb[:, i : i + 1],
+                in1=wgo_sb[:, c * CHUNK : (c + 1) * CHUNK],
+                op0=ALU.max,
+                op1=ALU.mult,
+            )
+            nc.vector.tensor_copy(pages[i][:].indirect(place_list[:, list_columns(c * CHUNK, CHUNK)]), weighted[:])
+
+        gather_pass0()
+        wb_q[0, 0] = quantise_weight("wb00", wb_raw[0, 0], PASS, nc.scalar.copy)
+        early_barge_words = keep("barge_word10", [P, HALF], U32)
+        early_boat_words = keep("boat_word10", [P, HALF], U32)
+        gather_pass1(0, early_boat_words[:], early_barge_words[:])
+        wb_q[1, 0] = quantise_weight("wb10", wb_raw[1, 0], PASS, nc.scalar.copy)
+        for a in range(PASSES):
+            wb_q[a, 1] = quantise_weight("wb%d1" % a, wb_raw[a, 1], PASS, nc.vector.tensor_copy)
+
+        units = [(2 * c + j, g) for c in range(CHUNKS) for g in range(PASSES) for j in range(CHUNK // P)]
+        units = units[:2] + [(2, 0)] + [unit for unit in units[2:] if unit != (2, 0)]
+        first_place = units.index((1, 1)) + 3
+        place_at = {first_place + n: divmod(n, PAGES) for n in range(2 * PAGES)}
+        place_at[len(units) - 1] = (CHUNKS - 2, 0)
+        wc_at = {units.index((0, 1)) + 1 + g: g for g in range(PASSES)}
+        for step in range(len(units) + 2):
+            if step < len(units):
+                products(*units[step])
+            if 1 <= step <= len(units):
+                difference(*units[step - 1])
+            if step >= 2:
+                make_z(*units[step - 2])
+            if step == 0:
+                late_words = keep("late_words", [P, 2 * HALF], U32, tag="late")
+                gather_pass1(1, late_words[:, :HALF], late_words[:, HALF:])
+            if step in wc_at:
+                g = wc_at[step]
+                wc_q[g] = quantise_weight("wc%d" % g, wc_raw[g], N, nc.vector.tensor_copy)
+            if step in place_at:
+                place(*place_at[step])
+
+        place_from_psum(CHUNKS - 2, 1)
+        place(CHUNKS - 1, 0)
+        place(CHUNKS - 1, 1)
+        last_two = keep("last_two", [P, 2 * CHUNK], F32)
+        for j in range(2):
+            floor_at_base(CHUNKS - 2 + j, 2, last_two[:, j * CHUNK : (j + 1) * CHUNK])
+        scatter(2, S - 2 * CHUNK, 2 * CHUNK, last_two[:])
+        for i in range(PAGES):
+            nc.sync.dma_start(out=out[i * P : (i + 1) * P, :], in_=pages[i][:])

from contextlib import ExitStack

import concourse.mybir as mybir
from concourse.masks import make_identity

K, H, N, T, S, T2 = 1024, 1024, 384, 4096, 1024, 2048
FLOPS = 2 * K * H * S * 2 + 2 * H * N * S

F32 = mybir.dt.float32
BF16 = mybir.dt.bfloat16
I32 = mybir.dt.int32
U32 = mybir.dt.uint32
U16 = mybir.dt.uint16
U8 = mybir.dt.uint8
FP8X4 = mybir.dt.float8_e4m3fn_x4
FP4X4 = mybir.dt.float4_e2m1fn_x4
ALU = mybir.AluOpType
ACT = mybir.ActivationFunctionType

P = 128
PACK = 4
PASS = P * PACK
PASSES = 2
HALF = S // 2
CHUNK = 256
CHUNKS = S // CHUNK
PAGES = N // P
PER_COLUMN = 16
STREAM_BUFS = 3
CHUNK_BUFS = 4


def tile_list_tow_plan_features_kernel(
    tc, tab_words, tab_scales, offs, offs2, offs3, wa_words, wa_scales, wb, gain, wc, base, wgo, out
):
    nc = tc.nc
    with ExitStack() as ctx:
        held = ctx.enter_context(tc.tile_pool(name="held", bufs=1))
        ring = ctx.enter_context(tc.tile_pool(name="ring", bufs=STREAM_BUFS))
        psum = ctx.enter_context(tc.psum_pool(name="psum", bufs=1))

        def keep(name, shape, dtype, tag=""):
            return held.tile(shape, dtype, name=name, tag=tag or name, align_bytes=64)

        def list_columns(first, count):
            return slice(first // PER_COLUMN, (first + count) // PER_COLUMN)

        barge_list = held.tile([P, S // PER_COLUMN], U16, name="barge_list")
        boat_list = held.tile([P, S // PER_COLUMN], U16, name="boat_list")
        place_list = held.tile([P, S // PER_COLUMN], U16, name="place_list")
        tab_scale = keep("tab_scale", [P, T], U8)
        wa_scale = keep("wa_scale", [P, PASSES, H], U8)
        barge_scale_pass1 = keep("barge_scale_pass1", [P, S], U8)

        warm_in = keep("warm_in", [P, 8], F32)
        warm_out = keep("warm_out", [P, 8], F32)
        nc.gpsimd.memset(warm_in[:], 0.0)
        nc.scalar.activation(out=warm_out[:], in_=warm_in[:], func=ACT.Silu)

        nc.vector.memset(tab_scale[:].bitcast(I32), 0)
        nc.sync.dma_start(barge_list[:], offs)
        nc.sync.dma_start(boat_list[:], offs2)
        nc.sync.dma_start(place_list[:], offs3)
        gain_sb = keep("gain_sb", [P, PASSES, PACK], F32)
        base_sb = keep("base_sb", [P, PAGES], F32)
        nc.vector.memset(wa_scale[:].bitcast(I32), 0)
        nc.vector.memset(barge_scale_pass1[:].bitcast(I32), 0)
        pages = [keep("page%d" % i, [P, T2], F32) for i in range(PAGES)]
        for page in pages:
            nc.vector.memset(page[:], 0.0)
        ident = keep("ident", [P, P], F32)
        make_identity(nc, ident[:])

        tab_word = [keep("tab_word%d" % a, [P, T], I32) for a in range(PASSES)]
        wb_raw = {(a, g): keep("wb_raw%d%d" % (a, g), [P, PACK, PASS], F32) for a, g in ((0, 0), (0, 1), (1, 1))}
        wb_raw[1, 0] = keep("wb_raw10", [P, PACK, PASS], F32, tag="late")
        wc_raw = [keep("wc_raw%d" % g, [P, PACK, N], F32) for g in range(PASSES)]
        wa_word = keep("wa_word", [P, PASSES, 2 * H], U8)
        wgo_sb = keep("wgo_sb", [P, S], F32)

        def load_tab_words(a):
            nc.sync.dma_start(out=tab_word[a][:], in_=tab_words[a].rearrange("p t i -> p (t i)").bitcast(I32))

        def load_wb(a, g):
            rows = wb[a * PASS : (a + 1) * PASS, g * PASS : (g + 1) * PASS]
            nc.sync.dma_start(out=wb_raw[a, g][:], in_=rows.rearrange("(p t) c -> p t c", t=PACK))

        def load_wa_scales(quadrants):
            for q in quadrants:
                nc.sync.dma_start(
                    out=wa_scale[32 * q : 32 * q + 4, :, :].bitcast(I32),
                    in_=wa_scales[:, 4 * q : 4 * q + 4, :].rearrange("a r c -> r a c").bitcast(I32),
                )

        for a in range(PASSES):
            for q in range(4):
                nc.sync.dma_start(
                    out=tab_scale[32 * q + 4 * a : 32 * q + 4 * a + 4, :].bitcast(I32),
                    in_=tab_scales[a, 4 * q : 4 * q + 4, :].bitcast(I32),
                )
        for a in range(PASSES):
            load_tab_words(a)
            load_wb(a, 0)
        load_wa_scales((0, 1))
        nc.sync.dma_start(out=wa_word[:].bitcast(I32), in_=wa_words.rearrange("a p c -> p a c").bitcast(I32))
        load_wa_scales((2, 3))
        load_wb(0, 1)
        nc.sync.dma_start(out=gain_sb[:], in_=gain.rearrange("(g p t) -> p g t", g=PASSES, t=PACK))
        load_wb(1, 1)
        for g in range(PASSES):
            rows = wc[g * PASS : (g + 1) * PASS, :]
            nc.sync.dma_start(out=wc_raw[g][:], in_=rows.rearrange("(p t) c -> p t c", t=PACK))
        with nc.allow_non_contiguous_dma(reason="one value of base to a partition and page"):
            nc.sync.dma_start(out=base_sb[:], in_=base.rearrange("(i p) -> p i", p=P))
        nc.sync.dma_start(out=wgo_sb[:], in_=wgo)

        barge_scale = keep("barge_scale", [P, S], U8)
        boat_scale = keep("boat_scale", [P, S], U8)
        nc.vector.tensor_copy(barge_scale[:], tab_scale[:].indirect(barge_list[:]))
        nc.vector.tensor_copy(boat_scale[:], tab_scale[:].indirect(boat_list[:]))
        for q in range(4):
            nc.scalar.dma_start(
                out=barge_scale_pass1[32 * q : 32 * q + 4, :].bitcast(I32),
                in_=barge_scale[32 * q + 4 : 32 * q + 8, :].bitcast(I32),
            )
        neg_base = keep("neg_base", [P, PAGES], F32)
        nc.scalar.activation(out=neg_base[:], in_=base_sb[:], func=ACT.Copy, scale=-1.0)

        barge_word = {}
        boat_word = {}

        def gather_pass0():
            for words, name, picks in ((boat_word, "boat", boat_list), (barge_word, "barge", barge_list)):
                whole = keep(name + "_word0", [P, S], U32)
                nc.vector.tensor_copy(whole[:], tab_word[0][:].bitcast(U32).indirect(picks[:]))
                words[0, 0] = whole[:, :HALF]
                words[0, 1] = whole[:, HALF:]

        def gather_pass1(h, boat_into, barge_into):
            window = tab_word[1][:].bitcast(U32)
            cols = list_columns(h * HALF, HALF)
            nc.vector.tensor_copy(boat_into, window.indirect(boat_list[:, cols]))
            nc.vector.tensor_copy(barge_into, window.indirect(barge_list[:, cols]))
            boat_word[1, h] = boat_into
            barge_word[1, h] = barge_into

        def quantise_weight(name, raw, width, copy):
            woven = ring.tile([P, PASS, PACK], BF16, name="woven", align_bytes=64)
            copy(
                out=woven[:, :width, :].rearrange("p (c i) t -> p c t i", i=4),
                in_=raw[:].rearrange("p t (c i) -> p c t i", i=4),
            )
            codes = keep(name + "_codes", [P, width], U32)
            scale = keep(name + "_scale", [P, width], U8)
            nc.vector.quantize_mx(
                out=codes[:].bitcast(FP8X4),
                scales=scale[:],
                in_=woven[:, :width, :].rearrange("p c t -> p (c t)"),
            )
            return codes, scale

        banks = {
            kind: [psum.tile([P, PASS], F32, name="%s%d" % (kind, b)) for b in range(count)]
            for kind, count in (("boat", 2), ("barge", 3), ("diff", 3))
        }
        taken = {kind: 0 for kind in banks}

        def next_bank(kind):
            taken[kind] = taken[kind] + 1
            return banks[kind][(taken[kind] - 1) % len(banks[kind])]

        wb_q = {}
        wc_q = {}
        bent = {}
        diffs = {}
        z_bf = {}
        z_q = {}

        def products(st, g):
            h, first = divmod(st * P, HALF)
            in_half = slice(first, first + P)
            entries = slice(st * P, (st + 1) * P)
            boat = next_bank("boat")
            for a in range(PASSES):
                codes, scale = wb_q[a, g]
                nc.tensor.matmul_mx(
                    out=boat[:],
                    lhsT=boat_word[a, h][:, in_half].bitcast(FP8X4),
                    lhsT_scale=boat_scale[4 * a : P, entries],
                    rhs=codes[:].bitcast(FP8X4),
                    rhs_scale=scale[:],
                    start=(a == 0),
                    stop=(a == PASSES - 1),
                )
            barge = next_bank("barge")
            for a, rows in enumerate((barge_scale, barge_scale_pass1)):
                nc.tensor.matmul_mx(
                    out=barge[:],
                    lhsT=barge_word[a, h][:, in_half].bitcast(FP8X4),
                    lhsT_scale=rows[:, entries],
                    rhs=wa_word[:, a, 2 * g * PASS : 2 * (g + 1) * PASS].bitcast(FP4X4),
                    rhs_scale=wa_scale[:, a, g * PASS : (g + 1) * PASS],
                    start=(a == 0),
                    stop=(a == PASSES - 1),
                )
            boat_by_slot = boat[:].rearrange("s (m t) -> s t m", t=PACK)
            barge_by_slot = barge[:].rearrange("s (m t) -> s t m", t=PACK)
            tanh_boat = ring.tile([P, PACK, P], F32, name="tanh_boat")
            nc.scalar.activation(out=tanh_boat[:], in_=boat_by_slot, func=ACT.Tanh)
            neg_sine = ring.tile([P, PACK, P], F32, name="neg_sine")
            nc.scalar.activation(out=neg_sine[:], in_=boat_by_slot, func=ACT.Sin, scale=-1.0)
            tanh_barge = ring.tile([P, PACK, P], F32, name="tanh_barge")
            nc.scalar.activation(out=tanh_barge[:], in_=barge_by_slot, func=ACT.Tanh)
            bent[st, g] = (tanh_barge, tanh_boat, neg_sine)

        def difference(st, g):
            tanh_barge, tanh_boat, neg_sine = bent[st, g]
            lead = ring.tile([P, PACK, P], F32, name="lead")
            nc.vector.tensor_tensor(out=lead[:], in0=tanh_barge[:], in1=tanh_boat[:], op=ALU.max)
            diff = next_bank("diff")[:].rearrange("p (t s) -> p t s", t=PACK)
            for i, term in enumerate((lead, neg_sine)):
                for t in range(PACK):
                    nc.tensor.matmul(
                        out=diff[:, t, :],
                        lhsT=term[:, t, :],
                        rhs=ident[:],
                        is_transpose=True,
                        start=(i == 0 and t == 0),
                        stop=(i == 1 and t == PACK - 1),
                    )
            diffs[st, g] = diff

        def make_z(st, g):
            c, j = divmod(st, CHUNK // P)
            if (c, g, j) == (CHUNKS - 1, PASSES - 1, 0):
                z_bf[c, g] = keep("last_z_bf", [P, CHUNK, PACK], BF16, tag="tail")
            elif j == 0:
                z_bf[c, g] = ring.tile([P, CHUNK, PACK], BF16, name="z_bf", align_bytes=64, bufs=CHUNK_BUFS)
            nc.vector.tensor_tensor(
                out=z_bf[c, g][:, j * P : (j + 1) * P, :],
                in0=diffs[st, g].rearrange("p t s -> p s t"),
                in1=gain_sb[:, g, :].unsqueeze(1).to_broadcast([P, P, PACK]),
                op=ALU.mult,
            )
            if j == CHUNK // P - 1:
                codes = ring.tile([P, CHUNK], U32, name="z_codes", align_bytes=64, bufs=CHUNK_BUFS)
                scale = ring.tile([P, CHUNK], U8, name="z_scale", align_bytes=64, bufs=CHUNK_BUFS)
                nc.vector.quantize_mx(
                    out=codes[:].bitcast(FP8X4),
                    scales=scale[:],
                    in_=z_bf[c, g][:].rearrange("p s t -> p (s t)"),
                )
                z_q[c, g] = (codes, scale)

        def last_product(c, i):
            y = next_bank("barge")[:, :CHUNK]
            for g in range(PASSES):
                w_codes, w_scale = wc_q[g]
                codes, scale = z_q[c, g]
                nc.tensor.matmul_mx(
                    out=y,
                    lhsT=w_codes[:, i * P : (i + 1) * P].bitcast(FP8X4),
                    lhsT_scale=w_scale[:, i * P : (i + 1) * P],
                    rhs=codes[:].bitcast(FP8X4),
                    rhs_scale=scale[:],
                    start=(g == 0),
                    stop=(g == PASSES - 1),
                )
            return y

        def floor_at_base(c, i, into):
            y = last_product(c, i)
            above = ring.tile([P, CHUNK], F32, name="above")
            nc.scalar.activation(out=above[:], in_=y, func=ACT.Relu, bias=neg_base[:, i : i + 1])
            nc.scalar.activation(out=into, in_=above[:], func=ACT.Identity, bias=base_sb[:, i : i + 1])

        def scatter(i, first, count, values):
            nc.vector.tensor_tensor(
                out=pages[i][:].indirect(place_list[:, list_columns(first, count)]),
                in0=values,
                in1=wgo_sb[:, first : first + count],
                op=ALU.mult,
            )

        def place(c, i):
            floored = ring.tile([P, CHUNK], F32, name="floored", bufs=CHUNK_BUFS)
            floor_at_base(c, i, floored[:])
            scatter(i, c * CHUNK, CHUNK, floored[:])

        def place_from_psum(c, i):
            y = last_product(c, i)
            weighted = keep("weighted", [P, CHUNK], F32, tag="tail")
            nc.vector.scalar_tensor_tensor(
                out=weighted[:],
                in0=y,
                scalar=base_sb[:, i : i + 1],
                in1=wgo_sb[:, c * CHUNK : (c + 1) * CHUNK],
                op0=ALU.max,
                op1=ALU.mult,
            )
            nc.vector.tensor_copy(pages[i][:].indirect(place_list[:, list_columns(c * CHUNK, CHUNK)]), weighted[:])

        gather_pass0()
        wb_q[0, 0] = quantise_weight("wb00", wb_raw[0, 0], PASS, nc.scalar.copy)
        early_barge_words = keep("barge_word10", [P, HALF], U32)
        early_boat_words = keep("boat_word10", [P, HALF], U32)
        gather_pass1(0, early_boat_words[:], early_barge_words[:])
        wb_q[1, 0] = quantise_weight("wb10", wb_raw[1, 0], PASS, nc.scalar.copy)
        for a in range(PASSES):
            wb_q[a, 1] = quantise_weight("wb%d1" % a, wb_raw[a, 1], PASS, nc.vector.tensor_copy)

        units = [(2 * c + j, g) for c in range(CHUNKS) for g in range(PASSES) for j in range(CHUNK // P)]
        units = units[:2] + [(2, 0)] + [unit for unit in units[2:] if unit != (2, 0)]
        first_place = units.index((1, 1)) + 3
        place_at = {first_place + n: divmod(n, PAGES) for n in range(2 * PAGES)}
        place_at[len(units) - 1] = (CHUNKS - 2, 0)
        wc_at = {units.index((0, 1)) + 1 + g: g for g in range(PASSES)}
        for step in range(len(units) + 2):
            if step < len(units):
                products(*units[step])
            if 1 <= step <= len(units):
                difference(*units[step - 1])
            if step >= 2:
                make_z(*units[step - 2])
            if step == 0:
                late_words = keep("late_words", [P, 2 * HALF], U32, tag="late")
                gather_pass1(1, late_words[:, :HALF], late_words[:, HALF:])
            if step in wc_at:
                g = wc_at[step]
                wc_q[g] = quantise_weight("wc%d" % g, wc_raw[g], N, nc.vector.tensor_copy)
            if step in place_at:
                place(*place_at[step])

        place_from_psum(CHUNKS - 2, 1)
        place(CHUNKS - 1, 0)
        place(CHUNKS - 1, 1)
        last_two = keep("last_two", [P, 2 * CHUNK], F32)
        for j in range(2):
            floor_at_base(CHUNKS - 2 + j, 2, last_two[:, j * CHUNK : (j + 1) * CHUNK])
        scatter(2, S - 2 * CHUNK, 2 * CHUNK, last_two[:])
        for i in range(PAGES):
            nc.sync.dma_start(out=out[i * P : (i + 1) * P, :], in_=pages[i][:])
